import numpy as np
import ml_dtypes

BF16 = ml_dtypes.bfloat16


def bf(x):
    return np.asarray(x, np.float32).astype(BF16)


def f32(x):
    return np.asarray(x, np.float32)


def f64(x):
    return np.asarray(x).astype(np.float64)


def striped(idx):
    return np.tile(idx.reshape(-1, 16).T, (8, 1))


S, K, M, N, E, Q = 256, 256, 256, 512, 4, 128


def sigmoid(v):
    return 1.0 / (1.0 + np.exp(-v))


def two_experts():
    first = np.random.permutation(S).reshape(E, S // E)
    return np.concatenate([np.random.permutation(np.concatenate([first[e], first[(e + 1) % E]])) for e in range(E)])


def setup_inputs():
    return {"table": bf(np.random.standard_normal((K, S))), "w": bf(np.random.standard_normal((E, K, M)) / np.sqrt(K)), "b": f32(0.5 * np.random.standard_normal((M, 1))), "offs": striped(two_experts())}


def reference(table, w, b, offs):
    idx = offs[:16].T.reshape(-1)
    x = f64(table)[:, idx]
    y = np.concatenate([f64(w)[e].T @ x[:, e * Q : (e + 1) * Q] for e in range(E)], axis=1)
    return (y + f64(b)) * sigmoid(y + f64(b))

@@ -1,0 +1,57 @@
+import concourse.mybir as mybir
+
+BF16, F32, U16 = mybir.dt.bfloat16, mybir.dt.float32, mybir.dt.uint16
+SILU = mybir.ActivationFunctionType.Silu
+
+P = 128
+TOKENS = 256
+FEATURES = 256
+OUT_FEATURES = 256
+EXPERTS = 4
+PIECE = 128
+K_BLOCKS = FEATURES // P
+M_BLOCKS = OUT_FEATURES // P
+PIECE_COLS = PIECE // 16
+
+FLOPS = 2 * FEATURES * OUT_FEATURES * EXPERTS * PIECE
+
+
+def tile_gather_matmul_kernel(tc, table, w, b, offs, out):
+    nc = tc.nc
+    with (
+        tc.tile_pool(name="held", bufs=1) as held,
+        tc.psum_pool(name="banks", bufs=1) as banks,
+    ):
+        offsets = held.tile([P, EXPERTS * PIECE_COLS], U16, name="offsets")
+        nc.sync.dma_start(offsets[:], offs)
+
+        table_blocks = [held.tile([P, TOKENS], BF16, name="table%d" % kb) for kb in range(K_BLOCKS)]
+        nc.sync.dma_start(table_blocks[0][:], table[0:P, :])
+        nc.scalar.dma_start(table_blocks[1][:], table[P : 2 * P, :])
+
+        weights = [held.tile([P, K_BLOCKS, OUT_FEATURES], BF16, name="weights%d" % e) for e in range(EXPERTS)]
+        for e in range(EXPERTS):
+            queue = nc.scalar if e % 2 == 0 else nc.sync
+            queue.dma_start(weights[e][:], w[e].rearrange("(kb p) m -> p kb m", p=P))
+
+        bias = held.tile([P, M_BLOCKS], F32, name="bias")
+        with nc.allow_non_contiguous_dma(reason="256 single values, one to a partition"):
+            nc.gpsimd.dma_start(bias[:], b.rearrange("(mb p) o -> p (mb o)", p=P))
+
+        out_blocks = out.rearrange("(mb p) j -> p mb j", p=P)
+
+        for e in range(EXPERTS):
+            piece = offsets[:, e * PIECE_COLS : (e + 1) * PIECE_COLS]
+            result = held.tile([P, M_BLOCKS, PIECE], F32, name="result%d" % e)
+            for mb in range(M_BLOCKS):
+                bank = banks.tile([P, PIECE], F32, name="bank%d_%d" % (e, mb))
+                for kb in range(K_BLOCKS):
+                    nc.tensor.matmul(
+                        bank[:],
+                        weights[e][:, kb, mb * P : (mb + 1) * P],
+                        table_blocks[kb][:].indirect(piece),
+                        start=(kb == 0),
+                        stop=(kb == K_BLOCKS - 1),
+                    )
+                nc.scalar.activation(result[:, mb, :], bank[:], SILU, bias=bias[:, mb : mb + 1])
+            nc.sync.dma_start(out_blocks[:, :, e * PIECE : (e + 1) * PIECE], result[:])

@@ -26,23 +26,23 @@ def tile_gather_matmul_kernel(tc, table, w, b, offs, out):
         nc.sync.dma_start(offsets[:], offs)
 
         table_blocks = [held.tile([P, TOKENS], BF16, name="table%d" % kb) for kb in range(K_BLOCKS)]
-        nc.sync.dma_start(table_blocks[0][:], table[0:P, :])
-        nc.scalar.dma_start(table_blocks[1][:], table[P : 2 * P, :])
+        for kb in range(K_BLOCKS):
+            nc.scalar.dma_start(table_blocks[kb][:], table[kb * P : (kb + 1) * P, :])
 
         weights = [held.tile([P, K_BLOCKS, OUT_FEATURES], BF16, name="weights%d" % e) for e in range(EXPERTS)]
         for e in range(EXPERTS):
-            queue = nc.scalar if e % 2 == 0 else nc.sync
-            queue.dma_start(weights[e][:], w[e].rearrange("(kb p) m -> p kb m", p=P))
+            nc.sync.dma_start(weights[e][:], w[e].rearrange("(kb p) m -> p kb m", p=P))
 
         bias = held.tile([P, M_BLOCKS], F32, name="bias")
         with nc.allow_non_contiguous_dma(reason="256 single values, one to a partition"):
-            nc.gpsimd.dma_start(bias[:], b.rearrange("(mb p) o -> p (mb o)", p=P))
+            nc.scalar.dma_start(bias[:], b.rearrange("(mb p) o -> p (mb o)", p=P))
 
-        out_blocks = out.rearrange("(mb p) j -> p mb j", p=P)
+        scratch = held.tile([P, 1], F32, name="scratch")
+        nc.vector.memset(scratch[:], 0.0)
+        nc.scalar.activation(scratch[:], scratch[:], SILU)
 
         for e in range(EXPERTS):
             piece = offsets[:, e * PIECE_COLS : (e + 1) * PIECE_COLS]
-            result = held.tile([P, M_BLOCKS, PIECE], F32, name="result%d" % e)
             for mb in range(M_BLOCKS):
                 bank = banks.tile([P, PIECE], F32, name="bank%d_%d" % (e, mb))
                 for kb in range(K_BLOCKS):
@@ -53,5 +53,6 @@ def tile_gather_matmul_kernel(tc, table, w, b, offs, out):
                         start=(kb == 0),
                         stop=(kb == K_BLOCKS - 1),
                     )
-                nc.scalar.activation(result[:, mb, :], bank[:], SILU, bias=bias[:, mb : mb + 1])
-            nc.sync.dma_start(out_blocks[:, :, e * PIECE : (e + 1) * PIECE], result[:])
+                result = held.tile([P, PIECE], F32, name="result%d_%d" % (e, mb))
+                nc.scalar.activation(result[:], bank[:], SILU, bias=bias[:, mb : mb + 1])
+                nc.sync.dma_start(out[mb * P : (mb + 1) * P, e * PIECE : (e + 1) * PIECE], result[:])

@@ -23,19 +23,18 @@ def tile_gather_matmul_kernel(tc, table, w, b, offs, out):
         tc.psum_pool(name="banks", bufs=1) as banks,
     ):
         offsets = held.tile([P, EXPERTS * PIECE_COLS], U16, name="offsets")
-        nc.sync.dma_start(offsets[:], offs)
-
         table_blocks = [held.tile([P, TOKENS], BF16, name="table%d" % kb) for kb in range(K_BLOCKS)]
-        for kb in range(K_BLOCKS):
-            nc.scalar.dma_start(table_blocks[kb][:], table[kb * P : (kb + 1) * P, :])
-
         weights = [held.tile([P, K_BLOCKS, OUT_FEATURES], BF16, name="weights%d" % e) for e in range(EXPERTS)]
-        for e in range(EXPERTS):
-            nc.sync.dma_start(weights[e][:], w[e].rearrange("(kb p) m -> p kb m", p=P))
-
         bias = held.tile([P, M_BLOCKS], F32, name="bias")
+
+        nc.sync.dma_start(offsets[:], offs)
+        nc.scalar.dma_start(table_blocks[0][:], table[0:P, :])
+        nc.sync.dma_start(weights[0][:], w[0].rearrange("(kb p) m -> p kb m", p=P))
         with nc.allow_non_contiguous_dma(reason="256 single values, one to a partition"):
             nc.scalar.dma_start(bias[:], b.rearrange("(mb p) o -> p (mb o)", p=P))
+        nc.sync.dma_start(table_blocks[1][:], table[P : 2 * P, :])
+        for e in range(1, EXPERTS):
+            nc.sync.dma_start(weights[e][:], w[e].rearrange("(kb p) m -> p kb m", p=P))
 
         scratch = held.tile([P, 1], F32, name="scratch")
         nc.vector.memset(scratch[:], 0.0)
@@ -43,16 +42,20 @@ def tile_gather_matmul_kernel(tc, table, w, b, offs, out):
 
         for e in range(EXPERTS):
             piece = offsets[:, e * PIECE_COLS : (e + 1) * PIECE_COLS]
+            bank = [banks.tile([P, PIECE], F32, name="bank%d_%d" % (e, mb)) for mb in range(M_BLOCKS)]
+            if e == 0:
+                order = [(kb, mb) for kb in range(K_BLOCKS) for mb in range(M_BLOCKS)]
+            else:
+                order = [(kb, mb) for mb in range(M_BLOCKS) for kb in range(K_BLOCKS)]
+            for kb, mb in order:
+                nc.tensor.matmul(
+                    bank[mb][:],
+                    weights[e][:, kb, mb * P : (mb + 1) * P],
+                    table_blocks[kb][:].indirect(piece),
+                    start=(kb == 0),
+                    stop=(kb == K_BLOCKS - 1),
+                )
             for mb in range(M_BLOCKS):
-                bank = banks.tile([P, PIECE], F32, name="bank%d_%d" % (e, mb))
-                for kb in range(K_BLOCKS):
-                    nc.tensor.matmul(
-                        bank[:],
-                        weights[e][:, kb, mb * P : (mb + 1) * P],
-                        table_blocks[kb][:].indirect(piece),
-                        start=(kb == 0),
-                        stop=(kb == K_BLOCKS - 1),
-                    )
                 result = held.tile([P, PIECE], F32, name="result%d_%d" % (e, mb))
-                nc.scalar.activation(result[:], bank[:], SILU, bias=bias[:, mb : mb + 1])
+                nc.scalar.activation(result[:], bank[mb][:], SILU, bias=bias[:, mb : mb + 1])
                 nc.sync.dma_start(out[mb * P : (mb + 1) * P, e * PIECE : (e + 1) * PIECE], result[:])

@@ -12,6 +12,7 @@ PIECE = 128
 K_BLOCKS = FEATURES // P
 M_BLOCKS = OUT_FEATURES // P
 PIECE_COLS = PIECE // 16
+ROW_ALIGN = 256
 
 FLOPS = 2 * FEATURES * OUT_FEATURES * EXPERTS * PIECE
 
@@ -23,8 +24,8 @@ def tile_gather_matmul_kernel(tc, table, w, b, offs, out):
         tc.psum_pool(name="banks", bufs=1) as banks,
     ):
         offsets = held.tile([P, EXPERTS * PIECE_COLS], U16, name="offsets")
-        table_blocks = [held.tile([P, TOKENS], BF16, name="table%d" % kb) for kb in range(K_BLOCKS)]
-        weights = [held.tile([P, K_BLOCKS, OUT_FEATURES], BF16, name="weights%d" % e) for e in range(EXPERTS)]
+        table_blocks = [held.tile([P, TOKENS], BF16, name="table%d" % kb, align_bytes=ROW_ALIGN) for kb in range(K_BLOCKS)]
+        weights = [held.tile([P, K_BLOCKS, OUT_FEATURES], BF16, name="weights%d" % e, align_bytes=ROW_ALIGN) for e in range(EXPERTS)]
         bias = held.tile([P, M_BLOCKS], F32, name="bias")
 
         nc.sync.dma_start(offsets[:], offs)
@@ -56,6 +57,6 @@ def tile_gather_matmul_kernel(tc, table, w, b, offs, out):
                     stop=(kb == K_BLOCKS - 1),
                 )
             for mb in range(M_BLOCKS):
-                result = held.tile([P, PIECE], F32, name="result%d_%d" % (e, mb))
+                result = held.tile([P, PIECE], F32, name="result%d_%d" % (e, mb), align_bytes=ROW_ALIGN)
                 nc.scalar.activation(result[:], bank[mb][:], SILU, bias=bias[:, mb : mb + 1])
                 nc.sync.dma_start(out[mb * P : (mb + 1) * P, e * PIECE : (e + 1) * PIECE], result[:])

@@ -26,13 +26,13 @@ def tile_gather_matmul_kernel(tc, table, w, b, offs, out):
         offsets = held.tile([P, EXPERTS * PIECE_COLS], U16, name="offsets")
         table_blocks = [held.tile([P, TOKENS], BF16, name="table%d" % kb, align_bytes=ROW_ALIGN) for kb in range(K_BLOCKS)]
         weights = [held.tile([P, K_BLOCKS, OUT_FEATURES], BF16, name="weights%d" % e, align_bytes=ROW_ALIGN) for e in range(EXPERTS)]
-        bias = held.tile([P, M_BLOCKS], F32, name="bias")
+        bias = held.tile([P, M_BLOCKS, 32 // 4], F32, name="bias")
 
         nc.sync.dma_start(offsets[:], offs)
         nc.scalar.dma_start(table_blocks[0][:], table[0:P, :])
         nc.sync.dma_start(weights[0][:], w[0].rearrange("(kb p) m -> p kb m", p=P))
         with nc.allow_non_contiguous_dma(reason="256 single values, one to a partition"):
-            nc.scalar.dma_start(bias[:], b.rearrange("(mb p) o -> p (mb o)", p=P))
+            nc.scalar.dma_start(bias[:, :, 0], b.rearrange("(mb p) o -> p (mb o)", p=P))
         nc.sync.dma_start(table_blocks[1][:], table[P : 2 * P, :])
         for e in range(1, EXPERTS):
             nc.sync.dma_start(weights[e][:], w[e].rearrange("(kb p) m -> p kb m", p=P))
@@ -58,5 +58,5 @@ def tile_gather_matmul_kernel(tc, table, w, b, offs, out):
                 )
             for mb in range(M_BLOCKS):
                 result = held.tile([P, PIECE], F32, name="result%d_%d" % (e, mb), align_bytes=ROW_ALIGN)
-                nc.scalar.activation(result[:], bank[mb][:], SILU, bias=bias[:, mb : mb + 1])
+                nc.scalar.activation(result[:], bank[mb][:], SILU, bias=bias[:, mb, 0:1])
                 nc.sync.dma_start(out[mb * P : (mb + 1) * P, e * PIECE : (e + 1) * PIECE], result[:])

@@ -26,13 +26,12 @@ def tile_gather_matmul_kernel(tc, table, w, b, offs, out):
         offsets = held.tile([P, EXPERTS * PIECE_COLS], U16, name="offsets")
         table_blocks = [held.tile([P, TOKENS], BF16, name="table%d" % kb, align_bytes=ROW_ALIGN) for kb in range(K_BLOCKS)]
         weights = [held.tile([P, K_BLOCKS, OUT_FEATURES], BF16, name="weights%d" % e, align_bytes=ROW_ALIGN) for e in range(EXPERTS)]
-        bias = held.tile([P, M_BLOCKS, 32 // 4], F32, name="bias")
+        bias = held.tile([P, M_BLOCKS], F32, name="bias")
 
         nc.sync.dma_start(offsets[:], offs)
         nc.scalar.dma_start(table_blocks[0][:], table[0:P, :])
         nc.sync.dma_start(weights[0][:], w[0].rearrange("(kb p) m -> p kb m", p=P))
-        with nc.allow_non_contiguous_dma(reason="256 single values, one to a partition"):
-            nc.scalar.dma_start(bias[:, :, 0], b.rearrange("(mb p) o -> p (mb o)", p=P))
+        nc.scalar.dma_start(bias[:], b.rearrange("(p mb) o -> p (mb o)", mb=M_BLOCKS))
         nc.sync.dma_start(table_blocks[1][:], table[P : 2 * P, :])
         for e in range(1, EXPERTS):
             nc.sync.dma_start(weights[e][:], w[e].rearrange("(kb p) m -> p kb m", p=P))
@@ -41,6 +40,7 @@ def tile_gather_matmul_kernel(tc, table, w, b, offs, out):
         nc.vector.memset(scratch[:], 0.0)
         nc.scalar.activation(scratch[:], scratch[:], SILU)
 
+        out_blocks = out.rearrange("(p mb) n -> mb p n", mb=M_BLOCKS)
         for e in range(EXPERTS):
             piece = offsets[:, e * PIECE_COLS : (e + 1) * PIECE_COLS]
             bank = [banks.tile([P, PIECE], F32, name="bank%d_%d" % (e, mb)) for mb in range(M_BLOCKS)]
@@ -51,12 +51,12 @@ def tile_gather_matmul_kernel(tc, table, w, b, offs, out):
             for kb, mb in order:
                 nc.tensor.matmul(
                     bank[mb][:],
-                    weights[e][:, kb, mb * P : (mb + 1) * P],
+                    weights[e][:, kb, mb:OUT_FEATURES:M_BLOCKS],
                     table_blocks[kb][:].indirect(piece),
                     start=(kb == 0),
                     stop=(kb == K_BLOCKS - 1),
                 )
             for mb in range(M_BLOCKS):
                 result = held.tile([P, PIECE], F32, name="result%d_%d" % (e, mb), align_bytes=ROW_ALIGN)
-                nc.scalar.activation(result[:], bank[mb][:], SILU, bias=bias[:, mb, 0:1])
-                nc.sync.dma_start(out[mb * P : (mb + 1) * P, e * PIECE : (e + 1) * PIECE], result[:])
+                nc.scalar.activation(result[:], bank[mb][:], SILU, bias=bias[:, mb : mb + 1])
+                nc.sync.dma_start(out_blocks[mb][:, e * PIECE : (e + 1) * PIECE], result[:])

@@ -24,17 +24,18 @@ def tile_gather_matmul_kernel(tc, table, w, b, offs, out):
         tc.psum_pool(name="banks", bufs=1) as banks,
     ):
         offsets = held.tile([P, EXPERTS * PIECE_COLS], U16, name="offsets")
-        table_blocks = [held.tile([P, TOKENS], BF16, name="table%d" % kb, align_bytes=ROW_ALIGN) for kb in range(K_BLOCKS)]
+        table_blocks = held.tile([P, K_BLOCKS, TOKENS], BF16, name="table_blocks", align_bytes=ROW_ALIGN)
         weights = [held.tile([P, K_BLOCKS, OUT_FEATURES], BF16, name="weights%d" % e, align_bytes=ROW_ALIGN) for e in range(EXPERTS)]
         bias = held.tile([P, M_BLOCKS], F32, name="bias")
 
+        first_matrix = w[0].rearrange("(p kb) m -> p kb m", kb=K_BLOCKS)
         nc.sync.dma_start(offsets[:], offs)
-        nc.scalar.dma_start(table_blocks[0][:], table[0:P, :])
-        nc.sync.dma_start(weights[0][:], w[0].rearrange("(kb p) m -> p kb m", p=P))
+        nc.scalar.dma_start(table_blocks[:], table.rearrange("(p kb) s -> p kb s", kb=K_BLOCKS))
+        nc.sync.dma_start(weights[0][:, 0, :], first_matrix[:, 0, :])
         nc.scalar.dma_start(bias[:], b.rearrange("(p mb) o -> p (mb o)", mb=M_BLOCKS))
-        nc.sync.dma_start(table_blocks[1][:], table[P : 2 * P, :])
+        nc.sync.dma_start(weights[0][:, 1, :], first_matrix[:, 1, :])
         for e in range(1, EXPERTS):
-            nc.sync.dma_start(weights[e][:], w[e].rearrange("(kb p) m -> p kb m", p=P))
+            nc.sync.dma_start(weights[e][:], w[e].rearrange("(p kb) m -> p kb m", kb=K_BLOCKS))
 
         scratch = held.tile([P, 1], F32, name="scratch")
         nc.vector.memset(scratch[:], 0.0)
@@ -52,7 +53,7 @@ def tile_gather_matmul_kernel(tc, table, w, b, offs, out):
                 nc.tensor.matmul(
                     bank[mb][:],
                     weights[e][:, kb, mb:OUT_FEATURES:M_BLOCKS],
-                    table_blocks[kb][:].indirect(piece),
+                    table_blocks[:, kb, :].indirect(piece),
                     start=(kb == 0),
                     stop=(kb == K_BLOCKS - 1),
                 )

@@ -26,7 +26,7 @@ def tile_gather_matmul_kernel(tc, table, w, b, offs, out):
         offsets = held.tile([P, EXPERTS * PIECE_COLS], U16, name="offsets")
         table_blocks = held.tile([P, K_BLOCKS, TOKENS], BF16, name="table_blocks", align_bytes=ROW_ALIGN)
         weights = [held.tile([P, K_BLOCKS, OUT_FEATURES], BF16, name="weights%d" % e, align_bytes=ROW_ALIGN) for e in range(EXPERTS)]
-        bias = held.tile([P, M_BLOCKS], F32, name="bias")
+        bias = held.tile([P, M_BLOCKS], F32, name="bias", align_bytes=ROW_ALIGN)
 
         first_matrix = w[0].rearrange("(p kb) m -> p kb m", kb=K_BLOCKS)
         nc.sync.dma_start(offsets[:], offs)

import concourse.mybir as mybir

BF16, F32, U16 = mybir.dt.bfloat16, mybir.dt.float32, mybir.dt.uint16
SILU = mybir.ActivationFunctionType.Silu

P = 128
TOKENS = 256
FEATURES = 256
OUT_FEATURES = 256
EXPERTS = 4
PIECE = 128
K_BLOCKS = FEATURES // P
M_BLOCKS = OUT_FEATURES // P
PIECE_COLS = PIECE // 16
ROW_ALIGN = 256

FLOPS = 2 * FEATURES * OUT_FEATURES * EXPERTS * PIECE


def tile_gather_matmul_kernel(tc, table, w, b, offs, out):
    nc = tc.nc
    with (
        tc.tile_pool(name="held", bufs=1) as held,
        tc.psum_pool(name="banks", bufs=1) as banks,
    ):
        offsets = held.tile([P, EXPERTS * PIECE_COLS], U16, name="offsets")
        table_blocks = held.tile([P, K_BLOCKS, TOKENS], BF16, name="table_blocks", align_bytes=ROW_ALIGN)
        weights = [held.tile([P, K_BLOCKS, OUT_FEATURES], BF16, name="weights%d" % e, align_bytes=ROW_ALIGN) for e in range(EXPERTS)]
        bias = held.tile([P, M_BLOCKS], F32, name="bias", align_bytes=ROW_ALIGN)

        first_matrix = w[0].rearrange("(p kb) m -> p kb m", kb=K_BLOCKS)
        nc.sync.dma_start(offsets[:], offs)
        nc.scalar.dma_start(table_blocks[:], table.rearrange("(p kb) s -> p kb s", kb=K_BLOCKS))
        nc.sync.dma_start(weights[0][:, 0, :], first_matrix[:, 0, :])
        nc.scalar.dma_start(bias[:], b.rearrange("(p mb) o -> p (mb o)", mb=M_BLOCKS))
        nc.sync.dma_start(weights[0][:, 1, :], first_matrix[:, 1, :])
        for e in range(1, EXPERTS):
            nc.sync.dma_start(weights[e][:], w[e].rearrange("(p kb) m -> p kb m", kb=K_BLOCKS))

        scratch = held.tile([P, 1], F32, name="scratch")
        nc.vector.memset(scratch[:], 0.0)
        nc.scalar.activation(scratch[:], scratch[:], SILU)

        out_blocks = out.rearrange("(p mb) n -> mb p n", mb=M_BLOCKS)
        for e in range(EXPERTS):
            piece = offsets[:, e * PIECE_COLS : (e + 1) * PIECE_COLS]
            bank = [banks.tile([P, PIECE], F32, name="bank%d_%d" % (e, mb)) for mb in range(M_BLOCKS)]
            if e == 0:
                order = [(kb, mb) for kb in range(K_BLOCKS) for mb in range(M_BLOCKS)]
            else:
                order = [(kb, mb) for mb in range(M_BLOCKS) for kb in range(K_BLOCKS)]
            for kb, mb in order:
                nc.tensor.matmul(
                    bank[mb][:],
                    weights[e][:, kb, mb:OUT_FEATURES:M_BLOCKS],
                    table_blocks[:, kb, :].indirect(piece),
                    start=(kb == 0),
                    stop=(kb == K_BLOCKS - 1),
                )
            for mb in range(M_BLOCKS):
                result = held.tile([P, PIECE], F32, name="result%d_%d" % (e, mb), align_bytes=ROW_ALIGN)
                nc.scalar.activation(result[:], bank[mb][:], SILU, bias=bias[:, mb : mb + 1])
                nc.sync.dma_start(out_blocks[mb][:, e * PIECE : (e + 1) * PIECE], result[:])
